import numpy as np
import ml_dtypes


def mxq(x, axis, fmt="e4m3"):
    dtype, down = {"e4m3": (ml_dtypes.float8_e4m3fn, 7), "e5m2": (ml_dtypes.float8_e5m2, 14)}[fmt]
    v = np.moveaxis(np.asarray(x, np.float32).astype(ml_dtypes.bfloat16).astype(np.float64), axis, -1)
    blocks = v.reshape(v.shape[:-1] + (-1, 32))
    amax = np.abs(blocks).max(-1, keepdims=True)
    byte = np.maximum(np.where(amax > 0, np.frexp(amax)[1] - 1 + 127, 0) - down, 1)
    scale = np.exp2(byte - 127.0)
    codes = (blocks / scale).astype(np.float32).astype(dtype).astype(np.float64)
    return np.moveaxis((codes * scale).reshape(v.shape), -1, axis)


WIDE = False


def mx_kscale(k):
    if not WIDE:
        return np.ones(k)
    levels = np.array([30, -30])
    if k % 512:
        return np.exp2(np.random.permutation(np.resize(levels, k // 32))).repeat(32)
    a = np.empty((k // 512, 16))
    for p in range(k // 512):
        a[p, :8] = np.random.permutation(np.resize(levels, 8))
        for g in range(8):
            far = levels[np.abs(levels - a[p, g]) >= 10]
            a[p, g + 8] = far[np.random.randint(len(far))]
    return np.exp2(a.ravel()).repeat(32)


def f64(x):
    return np.asarray(x).astype(np.float64)


def striped(idx):
    return np.tile(np.asarray(idx).reshape(-1, 16).T, (8, 1)).astype(np.uint16)


def unstriped(offs):
    return offs[:16].T.reshape(-1).astype(np.int64)


E2M1 = np.array([0.0, 0.5, 1.0, 1.5, 2.0, 3.0, 4.0, 6.0, -0.0, -0.5, -1.0, -1.5, -2.0, -3.0, -4.0, -6.0])


def pack_weight(w, fmt):
    k, n = w.shape
    w = f64(np.asarray(w, np.float32).astype(ml_dtypes.bfloat16)).reshape(k // 32, 32, n)
    amax = np.abs(w).max(1)
    if fmt in ("e4m3", "e5m2"):
        byte = np.frexp(amax)[1] - 1 + 127 - (7 if fmt == "e4m3" else 14)
    else:
        mant, ex = np.frexp(amax / 6.0)
        byte = np.where(mant > 0.5, ex, ex - 1) + 127
    byte = np.clip(np.where(amax > 0, byte, 1), 1, 254)
    scaled = (w * np.exp2(127.0 - byte)[:, None, :]).reshape(k, n).astype(np.float32)
    by_word = np.ascontiguousarray(scaled.reshape(k // 512, 128, 4, n).transpose(0, 1, 3, 2))
    if fmt in ("e4m3", "e5m2"):
        words = by_word.astype(ml_dtypes.float8_e4m3fn if fmt == "e4m3" else ml_dtypes.float8_e5m2).view(np.uint8)
    else:
        c = by_word.astype(ml_dtypes.float4_e2m1fn).view(np.uint8) & 0xF
        words = (c[..., 0::2] | (c[..., 1::2] << 4)).reshape(k // 512, 128, 2 * n)
    return np.ascontiguousarray(words), np.ascontiguousarray(byte.astype(np.uint8).reshape(k // 512, 16, n))


def unpack_weight(words, scales, fmt):
    g, _, n = scales.shape
    words = np.ascontiguousarray(words).reshape(g, 128, n, -1)
    if fmt in ("e4m3", "e5m2"):
        vals = words.view(ml_dtypes.float8_e4m3fn if fmt == "e4m3" else ml_dtypes.float8_e5m2).astype(np.float64)
    else:
        nib = np.empty((g, 128, n, 4), np.uint8)
        nib[..., 0::2] = words & 0xF
        nib[..., 1::2] = words >> 4
        vals = E2M1[nib]
    vals = vals * np.repeat(np.exp2(scales.astype(np.float64) - 127.0), 8, axis=1)[..., None]
    return vals.transpose(0, 1, 3, 2).reshape(g * 512, n)


K, T, J, I, R, Q = 512, 512, 256, 256, 512, 512


def setup_inputs():
    n = np.random.standard_normal
    idx = np.random.permutation(T)[:J]
    idx2 = np.random.permutation(T)[:I]
    idx3 = np.random.permutation(Q)[:I]
    fk = mx_kscale(K)
    fr = mx_kscale(R)
    xtp = pack_weight(n((K, T)) / fk[:, None], "e5m2")
    wap = pack_weight(n((K, R)) * 0.5 / np.sqrt(K) * fk[:, None] * fr, "e4m3")
    wbp = pack_weight(n((K, R)) * 1 / np.sqrt(K) * fk[:, None] / fr, "e2m1")
    return {
        "xt_words": xtp[0],
        "xt_scales": xtp[1],
        "wa_words": wap[0],
        "wa_scales": wap[1],
        "wb_words": wbp[0],
        "wb_scales": wbp[1],
        "ob": (n((R, I)) * 0.5 / fr[:, None]).astype(np.float32),
        "tv": (1.0 * n((J, Q))).astype(np.float32),
        "offs": striped(idx),
        "offs2": striped(idx2),
        "offs3": striped(idx3),
    }


def reference(xt_words, xt_scales, wa_words, wa_scales, wb_words, wb_scales, ob, tv, offs, offs2, offs3):
    idx = unstriped(offs)
    idx2 = unstriped(offs2)
    idx3 = unstriped(offs3)
    xtu = unpack_weight(xt_words, xt_scales, "e5m2")
    wau = unpack_weight(wa_words, wa_scales, "e4m3")
    wbu = unpack_weight(wb_words, wb_scales, "e2m1")
    xtidxg = xtu[:, idx]
    za = wau.T @ xtidxg
    ka1 = np.max(za, axis=1, keepdims=True)
    ha = np.maximum(za - 0.4 * ka1, 0.0)
    xtidx2g = xtu[:, idx2]
    zb = wbu.T @ xtidx2g
    hb = np.maximum(zb, f64(ob))
    haq = mxq(ha, 0, "e5m2")
    hbq = mxq(hb, 0, "e4m3")
    a0 = haq.T @ hbq
    y = np.tanh(0.04 * a0) * f64(tv)[:, idx3]
    return y

@@ -1,0 +1,183 @@
+from contextlib import ExitStack
+
+import concourse.mybir as mybir
+
+K, T, J, I, R, Q = 512, 512, 256, 256, 512, 512
+FLOPS = 2 * K * R * J + 2 * K * R * I + 2 * R * J * I
+
+F32 = mybir.dt.float32
+BF16 = mybir.dt.bfloat16
+I32 = mybir.dt.int32
+U32 = mybir.dt.uint32
+U16 = mybir.dt.uint16
+U8 = mybir.dt.uint8
+E4M3 = mybir.dt.float8_e4m3fn_x4
+E5M2 = mybir.dt.float8_e5m2_x4
+E2M1 = mybir.dt.float4_e2m1fn_x4
+ALU = mybir.AluOpType
+ACT = mybir.ActivationFunctionType
+
+P = 128
+PACK = 4
+RUN = 8
+BLOCKS = 16
+
+
+def load_scale_rows(queue, plane, scales):
+    for quad in range(4):
+        rows = scales[0, 4 * quad : 4 * quad + 4, :].bitcast(I32)
+        queue.dma_start(
+            out=plane[32 * quad : 32 * quad + 32, :].bitcast(I32),
+            in_=rows.unsqueeze(0).broadcast_to([8, 4, T // 4]),
+        )
+
+
+def deal_columns(nc, dealt, raw):
+    nc.scalar.copy(
+        out=dealt.bitcast(U32).rearrange("p (t b w) -> p t b w", t=PACK, b=BLOCKS),
+        in_=raw.bitcast(U32).rearrange("p (b t w) -> p t b w", t=PACK, b=BLOCKS),
+    )
+
+
+def tile_list_meet_peakgated_added_tabled_kernel(
+    tc, xt_words, xt_scales, wa_words, wa_scales, wb_words, wb_scales, ob, tv, offs, offs2, offs3, out
+):
+    nc = tc.nc
+    with ExitStack() as ctx:
+        sb = ctx.enter_context(tc.tile_pool(name="sb", bufs=1))
+        ps = ctx.enter_context(tc.psum_pool(name="ps", bufs=1))
+
+        list_a = sb.tile([P, J // 16], U16, name="list_a")
+        list_b = sb.tile([P, I // 16], U16, name="list_b")
+        list_v = sb.tile([P, I // 16], U16, name="list_v")
+        x_words = sb.tile([P, T], I32, name="x_words", align_bytes=64)
+        x_plane = sb.tile([P, T], U8, name="x_plane", align_bytes=64)
+        wa_raw = sb.tile([P, R], I32, name="wa_raw", align_bytes=64)
+        wa_raw_plane = sb.tile([P, R], U8, name="wa_raw_plane", align_bytes=64)
+        wb_raw = sb.tile([P, 2 * R], U8, name="wb_raw", align_bytes=64)
+        wb_raw_plane = sb.tile([P, R], U8, name="wb_raw_plane", align_bytes=64)
+        own = sb.tile([P, PACK, I], F32, name="own", align_bytes=64)
+        table = sb.tile([P, 2, Q], F32, name="table", align_bytes=64)
+
+        nc.sync.dma_start(list_a[:], offs)
+        nc.sync.dma_start(out=x_words[:], in_=xt_words[0].rearrange("p n t -> p (n t)").bitcast(I32))
+        load_scale_rows(nc.sync, x_plane, xt_scales)
+        nc.sync.dma_start(list_b[:], offs2)
+        nc.sync.dma_start(out=wa_raw[:], in_=wa_words[0].rearrange("p n t -> p (n t)").bitcast(I32))
+        load_scale_rows(nc.sync, wa_raw_plane, wa_scales)
+        nc.sync.dma_start(out=wb_raw[:].bitcast(I32), in_=wb_words[0].bitcast(I32))
+        load_scale_rows(nc.sync, wb_raw_plane, wb_scales)
+        ob_dealt = ob.rearrange("(b t q) i -> t b q i", t=PACK, q=RUN)
+        for t in range(PACK):
+            nc.sync.dma_start(out=own[:, t, :], in_=ob_dealt[t])
+        nc.sync.dma_start(out=table[:], in_=tv.rearrange("(h p) q -> p h q", p=P))
+        nc.sync.dma_start(list_v[:], offs3)
+
+        xa = sb.tile([P, J], U32, name="xa", align_bytes=64)
+        xa_plane = sb.tile([P, J], U8, name="xa_plane", align_bytes=64)
+        xb = sb.tile([P, I], U32, name="xb", align_bytes=64)
+        xb_plane = sb.tile([P, I], U8, name="xb_plane", align_bytes=64)
+        nc.vector.tensor_copy(xa[:], x_words[:].bitcast(U32).indirect(list_a[:]))
+        nc.vector.tensor_copy(xa_plane[:], x_plane[:].indirect(list_a[:]))
+        nc.vector.tensor_copy(xb[:], x_words[:].bitcast(U32).indirect(list_b[:]))
+        nc.vector.tensor_copy(xb_plane[:], x_plane[:].indirect(list_b[:]))
+
+        wa = sb.tile([P, R], U32, name="wa", align_bytes=64)
+        wa_plane = sb.tile([P, R], U8, name="wa_plane", align_bytes=64)
+        wb = sb.tile([P, 2 * R], U8, name="wb", align_bytes=64)
+        wb_plane = sb.tile([P, R], U8, name="wb_plane", align_bytes=64)
+        deal_columns(nc, wa[:], wa_raw[:])
+        deal_columns(nc, wa_plane[:], wa_raw_plane[:])
+        deal_columns(nc, wb[:], wb_raw[:])
+        deal_columns(nc, wb_plane[:], wb_raw_plane[:])
+
+        za = [ps.tile([P, J], F32, name=f"za{t}") for t in range(PACK)]
+        for t in range(PACK):
+            cols = slice(P * t, P * (t + 1))
+            nc.tensor.matmul_mx(
+                out=za[t][:],
+                lhsT=wa[:, cols].bitcast(E4M3),
+                lhsT_scale=wa_plane[:, cols],
+                rhs=xa[:].bitcast(E5M2),
+                rhs_scale=xa_plane[:],
+                start=True,
+                stop=True,
+            )
+        zb = [ps.tile([P, PACK, P], F32, name=f"zb{h}") for h in range(2)]
+        for h in range(2):
+            half = slice(P * h, P * (h + 1))
+            for t in range(PACK):
+                nc.tensor.matmul_mx(
+                    out=zb[h][:, t, :],
+                    lhsT=wb[:, 2 * P * t : 2 * P * (t + 1)].bitcast(E2M1),
+                    lhsT_scale=wb_plane[:, P * t : P * (t + 1)],
+                    rhs=xb[:, half].bitcast(E5M2),
+                    rhs_scale=xb_plane[:, half],
+                    start=True,
+                    stop=True,
+                )
+
+        shift = sb.tile([P, PACK], F32, name="shift")
+        scaled = sb.tile([P, PACK, J], F32, name="scaled")
+        ha_rows = sb.tile([P, PACK, J], BF16, name="ha_rows", align_bytes=64)
+        for t in range(PACK):
+            nc.vector.tensor_scalar(
+                out=scaled[:, t, :],
+                in0=za[t][:],
+                scalar1=-0.4,
+                scalar2=None,
+                op0=ALU.mult,
+                op1=ALU.min,
+                accum_out=shift[:, t : t + 1],
+            )
+            nc.scalar.activation(out=ha_rows[:, t, :], in_=za[t][:], func=ACT.Relu, bias=shift[:, t : t + 1])
+
+        hb = sb.tile([P, I, PACK], BF16, name="hb", align_bytes=64)
+        for h in range(2):
+            half = slice(P * h, P * (h + 1))
+            nc.vector.tensor_tensor(
+                out=hb[:, half, :].rearrange("p (c i) t -> p c t i", i=4),
+                in0=zb[h][:].rearrange("p t (c i) -> p c t i", i=4),
+                in1=own[:, :, half].rearrange("p t (c i) -> p c t i", i=4),
+                op=ALU.max,
+            )
+        hb_codes = sb.tile([P, I], U32, name="hb_codes", align_bytes=64)
+        hb_plane = sb.tile([P, I], U8, name="hb_plane", align_bytes=64)
+
+        ha = [sb.tile([P, P, PACK], BF16, name=f"ha{h}", align_bytes=64) for h in range(2)]
+        ha_codes = [sb.tile([P, P], U32, name=f"ha_codes{h}", align_bytes=64) for h in range(2)]
+        ha_plane = [sb.tile([P, P], U8, name=f"ha_plane{h}", align_bytes=64) for h in range(2)]
+        for h in range(2):
+            half = slice(P * h, P * (h + 1))
+            nc.vector.tensor_copy(
+                out=ha[h][:].rearrange("p (c i) t -> p c t i", i=4),
+                in_=ha_rows[:, :, half].rearrange("p t (c i) -> p c t i", i=4),
+            )
+        nc.vector.quantize_mx(
+            out=hb_codes[:].bitcast(E4M3), scales=hb_plane[:], in_=hb[:].rearrange("p i t -> p (i t)")
+        )
+        for h in range(2):
+            nc.vector.quantize_mx(
+                out=ha_codes[h][:].bitcast(E5M2), scales=ha_plane[h][:], in_=ha[h][:].rearrange("p j t -> p (j t)")
+            )
+
+        factor = sb.tile([P, 2, I], F32, name="factor")
+        for h in range(2):
+            nc.scalar.activation(out=factor[:, h, :], in_=table[:, h, :].indirect(list_v[:]), func=ACT.Copy)
+
+        score = [ps.tile([P, I], F32, name=f"score{h}") for h in range(2)]
+        squashed = sb.tile([P, 2, I], F32, name="squashed")
+        result = sb.tile([P, 2, I], F32, name="result")
+        for h in range(2):
+            nc.tensor.matmul_mx(
+                out=score[h][:],
+                lhsT=ha_codes[h][:].bitcast(E5M2),
+                lhsT_scale=ha_plane[h][:],
+                rhs=hb_codes[:].bitcast(E4M3),
+                rhs_scale=hb_plane[:],
+                start=True,
+                stop=True,
+            )
+            nc.scalar.activation(out=squashed[:, h, :], in_=score[h][:], func=ACT.Tanh, scale=0.04)
+            nc.vector.tensor_tensor(out=result[:, h, :], in0=squashed[:, h, :], in1=factor[:, h, :], op=ALU.mult)
+            nc.sync.dma_start(out=out[P * h : P * (h + 1), :], in_=result[:, h, :])

@@ -23,8 +23,8 @@ RUN = 8
 BLOCKS = 16
 
 
-def load_scale_rows(queue, plane, scales):
-    for quad in range(4):
+def load_scale_rows(queue, plane, scales, quads=range(4)):
+    for quad in quads:
         rows = scales[0, 4 * quad : 4 * quad + 4, :].bitcast(I32)
         queue.dma_start(
             out=plane[32 * quad : 32 * quad + 32, :].bitcast(I32),
@@ -55,32 +55,34 @@ def tile_list_meet_peakgated_added_tabled_kernel(
         wa_raw = sb.tile([P, R], I32, name="wa_raw", align_bytes=64)
         wa_raw_plane = sb.tile([P, R], U8, name="wa_raw_plane", align_bytes=64)
         wb_raw = sb.tile([P, 2 * R], U8, name="wb_raw", align_bytes=64)
-        wb_raw_plane = sb.tile([P, R], U8, name="wb_raw_plane", align_bytes=64)
-        own = sb.tile([P, PACK, I], F32, name="own", align_bytes=64)
+        wb_raw_plane = sb.tile([P, R], U8, name="wb_raw_plane", tag="wb_raw_plane", align_bytes=64)
+        own = sb.tile([P, PACK, I], F32, name="own", tag="own", align_bytes=64)
         table = sb.tile([P, 2, Q], F32, name="table", align_bytes=64)
 
         nc.sync.dma_start(list_a[:], offs)
+        load_scale_rows(nc.scalar, x_plane, xt_scales, range(2))
+        load_scale_rows(nc.sync, x_plane, xt_scales, range(2, 4))
         nc.sync.dma_start(out=x_words[:], in_=xt_words[0].rearrange("p n t -> p (n t)").bitcast(I32))
-        load_scale_rows(nc.sync, x_plane, xt_scales)
         nc.sync.dma_start(list_b[:], offs2)
         nc.sync.dma_start(out=wa_raw[:], in_=wa_words[0].rearrange("p n t -> p (n t)").bitcast(I32))
         load_scale_rows(nc.sync, wa_raw_plane, wa_scales)
+        load_scale_rows(nc.gpsimd, wb_raw_plane, wb_scales, range(1))
         nc.sync.dma_start(out=wb_raw[:].bitcast(I32), in_=wb_words[0].bitcast(I32))
-        load_scale_rows(nc.sync, wb_raw_plane, wb_scales)
+        load_scale_rows(nc.sync, wb_raw_plane, wb_scales, range(1, 4))
         ob_dealt = ob.rearrange("(b t q) i -> t b q i", t=PACK, q=RUN)
         for t in range(PACK):
             nc.sync.dma_start(out=own[:, t, :], in_=ob_dealt[t])
-        nc.sync.dma_start(out=table[:], in_=tv.rearrange("(h p) q -> p h q", p=P))
         nc.sync.dma_start(list_v[:], offs3)
+        nc.sync.dma_start(out=table[:], in_=tv.rearrange("(h p) q -> p h q", p=P))
 
         xa = sb.tile([P, J], U32, name="xa", align_bytes=64)
         xa_plane = sb.tile([P, J], U8, name="xa_plane", align_bytes=64)
         xb = sb.tile([P, I], U32, name="xb", align_bytes=64)
         xb_plane = sb.tile([P, I], U8, name="xb_plane", align_bytes=64)
-        nc.vector.tensor_copy(xa[:], x_words[:].bitcast(U32).indirect(list_a[:]))
         nc.vector.tensor_copy(xa_plane[:], x_plane[:].indirect(list_a[:]))
-        nc.vector.tensor_copy(xb[:], x_words[:].bitcast(U32).indirect(list_b[:]))
+        nc.vector.tensor_copy(xa[:], x_words[:].bitcast(U32).indirect(list_a[:]))
         nc.vector.tensor_copy(xb_plane[:], x_plane[:].indirect(list_b[:]))
+        nc.vector.tensor_copy(xb[:], x_words[:].bitcast(U32).indirect(list_b[:]))
 
         wa = sb.tile([P, R], U32, name="wa", align_bytes=64)
         wa_plane = sb.tile([P, R], U8, name="wa_plane", align_bytes=64)
@@ -119,7 +121,7 @@ def tile_list_meet_peakgated_added_tabled_kernel(
 
         shift = sb.tile([P, PACK], F32, name="shift")
         scaled = sb.tile([P, PACK, J], F32, name="scaled")
-        ha_rows = sb.tile([P, PACK, J], BF16, name="ha_rows", align_bytes=64)
+        ha_rows = sb.tile([P, PACK, J], BF16, name="ha_rows", tag="wb_raw_plane", align_bytes=64)
         for t in range(PACK):
             nc.vector.tensor_scalar(
                 out=scaled[:, t, :],
@@ -132,52 +134,53 @@ def tile_list_meet_peakgated_added_tabled_kernel(
             )
             nc.scalar.activation(out=ha_rows[:, t, :], in_=za[t][:], func=ACT.Relu, bias=shift[:, t : t + 1])
 
-        hb = sb.tile([P, I, PACK], BF16, name="hb", align_bytes=64)
-        for h in range(2):
-            half = slice(P * h, P * (h + 1))
+        hb = [sb.tile([P, P, PACK], BF16, name=f"hb{g}", align_bytes=64) for g in range(2)]
+        hb_codes = [sb.tile([P, P], U32, name=f"hb_codes{g}", align_bytes=64) for g in range(2)]
+        hb_plane = [sb.tile([P, P], U8, name=f"hb_plane{g}", align_bytes=64) for g in range(2)]
+        ha_codes = sb.tile([P, 2, P], U32, name="ha_codes", tag="own", align_bytes=64)
+        ha_plane = [sb.tile([P, P], U8, name=f"ha_plane{h}", align_bytes=64) for h in range(2)]
+        for g in range(2):
             nc.vector.tensor_tensor(
-                out=hb[:, half, :].rearrange("p (c i) t -> p c t i", i=4),
-                in0=zb[h][:].rearrange("p t (c i) -> p c t i", i=4),
-                in1=own[:, :, half].rearrange("p t (c i) -> p c t i", i=4),
+                out=hb[g][:].rearrange("p (c i) t -> p c t i", i=4),
+                in0=zb[g][:].rearrange("p t (c i) -> p c t i", i=4),
+                in1=own[:, :, P * g : P * (g + 1)].rearrange("p t (c i) -> p c t i", i=4),
                 op=ALU.max,
             )
-        hb_codes = sb.tile([P, I], U32, name="hb_codes", align_bytes=64)
-        hb_plane = sb.tile([P, I], U8, name="hb_plane", align_bytes=64)
-
-        ha = [sb.tile([P, P, PACK], BF16, name=f"ha{h}", align_bytes=64) for h in range(2)]
-        ha_codes = [sb.tile([P, P], U32, name=f"ha_codes{h}", align_bytes=64) for h in range(2)]
-        ha_plane = [sb.tile([P, P], U8, name=f"ha_plane{h}", align_bytes=64) for h in range(2)]
+        ha = sb.tile([P, 2, P, PACK], BF16, name="ha", align_bytes=64)
         for h in range(2):
-            half = slice(P * h, P * (h + 1))
-            nc.vector.tensor_copy(
-                out=ha[h][:].rearrange("p (c i) t -> p c t i", i=4),
-                in_=ha_rows[:, :, half].rearrange("p t (c i) -> p c t i", i=4),
+            nc.scalar.copy(
+                out=ha[:, h].rearrange("p (c i) t -> p c t i", i=4),
+                in_=ha_rows[:, :, P * h : P * (h + 1)].rearrange("p t (c i) -> p c t i", i=4),
             )
-        nc.vector.quantize_mx(
-            out=hb_codes[:].bitcast(E4M3), scales=hb_plane[:], in_=hb[:].rearrange("p i t -> p (i t)")
-        )
         for h in range(2):
             nc.vector.quantize_mx(
-                out=ha_codes[h][:].bitcast(E5M2), scales=ha_plane[h][:], in_=ha[h][:].rearrange("p j t -> p (j t)")
+                out=hb_codes[h][:].bitcast(E4M3), scales=hb_plane[h][:], in_=hb[h][:].rearrange("p i t -> p (i t)")
+            )
+            nc.vector.quantize_mx(
+                out=ha_codes[:, h, :].bitcast(E5M2), scales=ha_plane[h][:], in_=ha[:, h].rearrange("p j t -> p (j t)")
             )
 
         factor = sb.tile([P, 2, I], F32, name="factor")
-        for h in range(2):
-            nc.scalar.activation(out=factor[:, h, :], in_=table[:, h, :].indirect(list_v[:]), func=ACT.Copy)
+        nc.vector.tensor_copy(factor[:, 0, :], table[:, 0, :].indirect(list_v[:]))
+        nc.scalar.activation(out=factor[:, 1, :], in_=table[:, 1, :].indirect(list_v[:]), func=ACT.Copy)
 
-        score = [ps.tile([P, I], F32, name=f"score{h}") for h in range(2)]
         squashed = sb.tile([P, 2, I], F32, name="squashed")
         result = sb.tile([P, 2, I], F32, name="result")
         for h in range(2):
-            nc.tensor.matmul_mx(
-                out=score[h][:],
-                lhsT=ha_codes[h][:].bitcast(E5M2),
-                lhsT_scale=ha_plane[h][:],
-                rhs=hb_codes[:].bitcast(E4M3),
-                rhs_scale=hb_plane[:],
-                start=True,
-                stop=True,
-            )
-            nc.scalar.activation(out=squashed[:, h, :], in_=score[h][:], func=ACT.Tanh, scale=0.04)
-            nc.vector.tensor_tensor(out=result[:, h, :], in0=squashed[:, h, :], in1=factor[:, h, :], op=ALU.mult)
+            for g in range(2):
+                cols = slice(P * g, P * (g + 1))
+                score = ps.tile([P, P], F32, name=f"za{2 * h + g}")
+                nc.tensor.matmul_mx(
+                    out=score[:],
+                    lhsT=ha_codes[:, h, :].bitcast(E5M2),
+                    lhsT_scale=ha_plane[h][:],
+                    rhs=hb_codes[g][:].bitcast(E4M3),
+                    rhs_scale=hb_plane[g][:],
+                    start=True,
+                    stop=True,
+                )
+                nc.scalar.activation(out=squashed[:, h, cols], in_=score[:], func=ACT.Tanh, scale=0.04)
+                nc.vector.tensor_tensor(
+                    out=result[:, h, cols], in0=squashed[:, h, cols], in1=factor[:, h, cols], op=ALU.mult
+                )
             nc.sync.dma_start(out=out[P * h : P * (h + 1), :], in_=result[:, h, :])

@@ -45,6 +45,7 @@ def tile_list_meet_peakgated_added_tabled_kernel(
     nc = tc.nc
     with ExitStack() as ctx:
         sb = ctx.enter_context(tc.tile_pool(name="sb", bufs=1))
+        shared = ctx.enter_context(tc.tile_pool(name="shared", bufs=1))
         ps = ctx.enter_context(tc.psum_pool(name="ps", bufs=1))
 
         list_a = sb.tile([P, J // 16], U16, name="list_a")
@@ -56,16 +57,16 @@ def tile_list_meet_peakgated_added_tabled_kernel(
         wa_raw_plane = sb.tile([P, R], U8, name="wa_raw_plane", align_bytes=64)
         wb_raw = sb.tile([P, 2 * R], U8, name="wb_raw", align_bytes=64)
         wb_raw_plane = sb.tile([P, R], U8, name="wb_raw_plane", tag="wb_raw_plane", align_bytes=64)
-        own = sb.tile([P, PACK, I], F32, name="own", tag="own", align_bytes=64)
-        table = sb.tile([P, 2, Q], F32, name="table", align_bytes=64)
+        own = shared.tile([P, PACK, I], F32, name="own", align_bytes=64, offset=0)
+        table = [sb.tile([P, Q], F32, name=f"table{h}", tag=f"table{h}", align_bytes=64) for h in range(2)]
 
         nc.sync.dma_start(list_a[:], offs)
-        load_scale_rows(nc.scalar, x_plane, xt_scales, range(2))
-        load_scale_rows(nc.sync, x_plane, xt_scales, range(2, 4))
+        load_scale_rows(nc.sync, x_plane, xt_scales)
         nc.sync.dma_start(out=x_words[:], in_=xt_words[0].rearrange("p n t -> p (n t)").bitcast(I32))
         nc.sync.dma_start(list_b[:], offs2)
         nc.sync.dma_start(out=wa_raw[:], in_=wa_words[0].rearrange("p n t -> p (n t)").bitcast(I32))
-        load_scale_rows(nc.sync, wa_raw_plane, wa_scales)
+        load_scale_rows(nc.gpsimd, wa_raw_plane, wa_scales, range(1))
+        load_scale_rows(nc.sync, wa_raw_plane, wa_scales, range(1, 4))
         load_scale_rows(nc.gpsimd, wb_raw_plane, wb_scales, range(1))
         nc.sync.dma_start(out=wb_raw[:].bitcast(I32), in_=wb_words[0].bitcast(I32))
         load_scale_rows(nc.sync, wb_raw_plane, wb_scales, range(1, 4))
@@ -73,7 +74,8 @@ def tile_list_meet_peakgated_added_tabled_kernel(
         for t in range(PACK):
             nc.sync.dma_start(out=own[:, t, :], in_=ob_dealt[t])
         nc.sync.dma_start(list_v[:], offs3)
-        nc.sync.dma_start(out=table[:], in_=tv.rearrange("(h p) q -> p h q", p=P))
+        for h in (1, 0):
+            nc.sync.dma_start(out=table[h][:], in_=tv[P * h : P * (h + 1), :])
 
         xa = sb.tile([P, J], U32, name="xa", align_bytes=64)
         xa_plane = sb.tile([P, J], U8, name="xa_plane", align_bytes=64)
@@ -121,7 +123,7 @@ def tile_list_meet_peakgated_added_tabled_kernel(
 
         shift = sb.tile([P, PACK], F32, name="shift")
         scaled = sb.tile([P, PACK, J], F32, name="scaled")
-        ha_rows = sb.tile([P, PACK, J], BF16, name="ha_rows", tag="wb_raw_plane", align_bytes=64)
+        ha_pairs = sb.tile([P, 2, J, 2], BF16, name="ha_pairs", tag="wb_raw_plane", align_bytes=64)
         for t in range(PACK):
             nc.vector.tensor_scalar(
                 out=scaled[:, t, :],
@@ -132,12 +134,12 @@ def tile_list_meet_peakgated_added_tabled_kernel(
                 op1=ALU.min,
                 accum_out=shift[:, t : t + 1],
             )
-            nc.scalar.activation(out=ha_rows[:, t, :], in_=za[t][:], func=ACT.Relu, bias=shift[:, t : t + 1])
+            nc.scalar.activation(out=ha_pairs[:, t // 2, :, t % 2], in_=za[t][:], func=ACT.Relu, bias=shift[:, t : t + 1])
 
-        hb = [sb.tile([P, P, PACK], BF16, name=f"hb{g}", align_bytes=64) for g in range(2)]
+        hb = [sb.tile([P, P, PACK], BF16, name=f"hb{g}", tag=f"hb{g}", align_bytes=64) for g in range(2)]
         hb_codes = [sb.tile([P, P], U32, name=f"hb_codes{g}", align_bytes=64) for g in range(2)]
         hb_plane = [sb.tile([P, P], U8, name=f"hb_plane{g}", align_bytes=64) for g in range(2)]
-        ha_codes = sb.tile([P, 2, P], U32, name="ha_codes", tag="own", align_bytes=64)
+        ha_codes = shared.tile([P, 2, P], U32, name="ha_codes", align_bytes=64, offset=0)
         ha_plane = [sb.tile([P, P], U8, name=f"ha_plane{h}", align_bytes=64) for h in range(2)]
         for g in range(2):
             nc.vector.tensor_tensor(
@@ -146,26 +148,33 @@ def tile_list_meet_peakgated_added_tabled_kernel(
                 in1=own[:, :, P * g : P * (g + 1)].rearrange("p t (c i) -> p c t i", i=4),
                 op=ALU.max,
             )
-        ha = sb.tile([P, 2, P, PACK], BF16, name="ha", align_bytes=64)
-        for h in range(2):
-            nc.scalar.copy(
-                out=ha[:, h].rearrange("p (c i) t -> p c t i", i=4),
-                in_=ha_rows[:, :, P * h : P * (h + 1)].rearrange("p t (c i) -> p c t i", i=4),
+        ha = [
+            sb.tile([P, P * PACK], BF16, name="ha0", align_bytes=64),
+            shared.tile([P, P * PACK], BF16, name="ha1", align_bytes=64, offset=2048),
+        ]
+        pairs = ha_pairs[:].rearrange("p u j e -> p u (j e)")
+        for h, (copy, word) in enumerate(((nc.scalar.copy, U32), (nc.vector.tensor_copy, I32))):
+            copy(
+                out=ha[h][:].bitcast(word).rearrange("p (j u) -> p j u", u=2),
+                in_=pairs.bitcast(word)[:, :, P * h : P * (h + 1)].rearrange("p u j -> p j u"),
             )
         for h in range(2):
             nc.vector.quantize_mx(
                 out=hb_codes[h][:].bitcast(E4M3), scales=hb_plane[h][:], in_=hb[h][:].rearrange("p i t -> p (i t)")
             )
             nc.vector.quantize_mx(
-                out=ha_codes[:, h, :].bitcast(E5M2), scales=ha_plane[h][:], in_=ha[:, h].rearrange("p j t -> p (j t)")
+                out=ha_codes[:, h, :].bitcast(E5M2), scales=ha_plane[h][:], in_=ha[h][:]
             )
 
-        factor = sb.tile([P, 2, I], F32, name="factor")
-        nc.vector.tensor_copy(factor[:, 0, :], table[:, 0, :].indirect(list_v[:]))
-        nc.scalar.activation(out=factor[:, 1, :], in_=table[:, 1, :].indirect(list_v[:]), func=ACT.Copy)
+        factor = [
+            sb.tile([P, I], F32, name=f"factor{h}", tag=tag, align_bytes=64)
+            for h, tag in enumerate(("hb1", "factor1"))
+        ]
+        nc.vector.tensor_copy(factor[0][:], table[0][:].indirect(list_v[:]))
+        nc.scalar.activation(out=factor[1][:], in_=table[1][:].indirect(list_v[:]), func=ACT.Copy)
 
-        squashed = sb.tile([P, 2, I], F32, name="squashed")
-        result = sb.tile([P, 2, I], F32, name="result")
+        squashed = sb.tile([P, 2, I], F32, name="squashed", tag="table1", align_bytes=64)
+        result = sb.tile([P, 2, I], F32, name="result", tag="table0", align_bytes=64)
         for h in range(2):
             for g in range(2):
                 cols = slice(P * g, P * (g + 1))
@@ -181,6 +190,6 @@ def tile_list_meet_peakgated_added_tabled_kernel(
                 )
                 nc.scalar.activation(out=squashed[:, h, cols], in_=score[:], func=ACT.Tanh, scale=0.04)
                 nc.vector.tensor_tensor(
-                    out=result[:, h, cols], in0=squashed[:, h, cols], in1=factor[:, h, cols], op=ALU.mult
+                    out=result[:, h, cols], in0=squashed[:, h, cols], in1=factor[h][:, cols], op=ALU.mult
                 )
             nc.sync.dma_start(out=out[P * h : P * (h + 1), :], in_=result[:, h, :])

from contextlib import ExitStack

import concourse.mybir as mybir

K, T, J, I, R, Q = 512, 512, 256, 256, 512, 512
FLOPS = 2 * K * R * J + 2 * K * R * I + 2 * R * J * I

F32 = mybir.dt.float32
BF16 = mybir.dt.bfloat16
I32 = mybir.dt.int32
U32 = mybir.dt.uint32
U16 = mybir.dt.uint16
U8 = mybir.dt.uint8
E4M3 = mybir.dt.float8_e4m3fn_x4
E5M2 = mybir.dt.float8_e5m2_x4
E2M1 = mybir.dt.float4_e2m1fn_x4
ALU = mybir.AluOpType
ACT = mybir.ActivationFunctionType

P = 128
PACK = 4
RUN = 8
BLOCKS = 16


def load_scale_rows(queue, plane, scales, quads=range(4)):
    for quad in quads:
        rows = scales[0, 4 * quad : 4 * quad + 4, :].bitcast(I32)
        queue.dma_start(
            out=plane[32 * quad : 32 * quad + 32, :].bitcast(I32),
            in_=rows.unsqueeze(0).broadcast_to([8, 4, T // 4]),
        )


def deal_columns(nc, dealt, raw):
    nc.scalar.copy(
        out=dealt.bitcast(U32).rearrange("p (t b w) -> p t b w", t=PACK, b=BLOCKS),
        in_=raw.bitcast(U32).rearrange("p (b t w) -> p t b w", t=PACK, b=BLOCKS),
    )


def tile_list_meet_peakgated_added_tabled_kernel(
    tc, xt_words, xt_scales, wa_words, wa_scales, wb_words, wb_scales, ob, tv, offs, offs2, offs3, out
):
    nc = tc.nc
    with ExitStack() as ctx:
        sb = ctx.enter_context(tc.tile_pool(name="sb", bufs=1))
        shared = ctx.enter_context(tc.tile_pool(name="shared", bufs=1))
        ps = ctx.enter_context(tc.psum_pool(name="ps", bufs=1))

        list_a = sb.tile([P, J // 16], U16, name="list_a")
        list_b = sb.tile([P, I // 16], U16, name="list_b")
        list_v = sb.tile([P, I // 16], U16, name="list_v")
        x_words = sb.tile([P, T], I32, name="x_words", align_bytes=64)
        x_plane = sb.tile([P, T], U8, name="x_plane", align_bytes=64)
        wa_raw = sb.tile([P, R], I32, name="wa_raw", align_bytes=64)
        wa_raw_plane = sb.tile([P, R], U8, name="wa_raw_plane", align_bytes=64)
        wb_raw = sb.tile([P, 2 * R], U8, name="wb_raw", align_bytes=64)
        wb_raw_plane = sb.tile([P, R], U8, name="wb_raw_plane", tag="wb_raw_plane", align_bytes=64)
        own = shared.tile([P, PACK, I], F32, name="own", align_bytes=64, offset=0)
        table = [sb.tile([P, Q], F32, name=f"table{h}", tag=f"table{h}", align_bytes=64) for h in range(2)]

        nc.sync.dma_start(list_a[:], offs)
        load_scale_rows(nc.sync, x_plane, xt_scales)
        nc.sync.dma_start(out=x_words[:], in_=xt_words[0].rearrange("p n t -> p (n t)").bitcast(I32))
        nc.sync.dma_start(list_b[:], offs2)
        nc.sync.dma_start(out=wa_raw[:], in_=wa_words[0].rearrange("p n t -> p (n t)").bitcast(I32))
        load_scale_rows(nc.gpsimd, wa_raw_plane, wa_scales, range(1))
        load_scale_rows(nc.sync, wa_raw_plane, wa_scales, range(1, 4))
        load_scale_rows(nc.gpsimd, wb_raw_plane, wb_scales, range(1))
        nc.sync.dma_start(out=wb_raw[:].bitcast(I32), in_=wb_words[0].bitcast(I32))
        load_scale_rows(nc.sync, wb_raw_plane, wb_scales, range(1, 4))
        ob_dealt = ob.rearrange("(b t q) i -> t b q i", t=PACK, q=RUN)
        for t in range(PACK):
            nc.sync.dma_start(out=own[:, t, :], in_=ob_dealt[t])
        nc.sync.dma_start(list_v[:], offs3)
        for h in (1, 0):
            nc.sync.dma_start(out=table[h][:], in_=tv[P * h : P * (h + 1), :])

        xa = sb.tile([P, J], U32, name="xa", align_bytes=64)
        xa_plane = sb.tile([P, J], U8, name="xa_plane", align_bytes=64)
        xb = sb.tile([P, I], U32, name="xb", align_bytes=64)
        xb_plane = sb.tile([P, I], U8, name="xb_plane", align_bytes=64)
        nc.vector.tensor_copy(xa_plane[:], x_plane[:].indirect(list_a[:]))
        nc.vector.tensor_copy(xa[:], x_words[:].bitcast(U32).indirect(list_a[:]))
        nc.vector.tensor_copy(xb_plane[:], x_plane[:].indirect(list_b[:]))
        nc.vector.tensor_copy(xb[:], x_words[:].bitcast(U32).indirect(list_b[:]))

        wa = sb.tile([P, R], U32, name="wa", align_bytes=64)
        wa_plane = sb.tile([P, R], U8, name="wa_plane", align_bytes=64)
        wb = sb.tile([P, 2 * R], U8, name="wb", align_bytes=64)
        wb_plane = sb.tile([P, R], U8, name="wb_plane", align_bytes=64)
        deal_columns(nc, wa[:], wa_raw[:])
        deal_columns(nc, wa_plane[:], wa_raw_plane[:])
        deal_columns(nc, wb[:], wb_raw[:])
        deal_columns(nc, wb_plane[:], wb_raw_plane[:])

        za = [ps.tile([P, J], F32, name=f"za{t}") for t in range(PACK)]
        for t in range(PACK):
            cols = slice(P * t, P * (t + 1))
            nc.tensor.matmul_mx(
                out=za[t][:],
                lhsT=wa[:, cols].bitcast(E4M3),
                lhsT_scale=wa_plane[:, cols],
                rhs=xa[:].bitcast(E5M2),
                rhs_scale=xa_plane[:],
                start=True,
                stop=True,
            )
        zb = [ps.tile([P, PACK, P], F32, name=f"zb{h}") for h in range(2)]
        for h in range(2):
            half = slice(P * h, P * (h + 1))
            for t in range(PACK):
                nc.tensor.matmul_mx(
                    out=zb[h][:, t, :],
                    lhsT=wb[:, 2 * P * t : 2 * P * (t + 1)].bitcast(E2M1),
                    lhsT_scale=wb_plane[:, P * t : P * (t + 1)],
                    rhs=xb[:, half].bitcast(E5M2),
                    rhs_scale=xb_plane[:, half],
                    start=True,
                    stop=True,
                )

        shift = sb.tile([P, PACK], F32, name="shift")
        scaled = sb.tile([P, PACK, J], F32, name="scaled")
        ha_pairs = sb.tile([P, 2, J, 2], BF16, name="ha_pairs", tag="wb_raw_plane", align_bytes=64)
        for t in range(PACK):
            nc.vector.tensor_scalar(
                out=scaled[:, t, :],
                in0=za[t][:],
                scalar1=-0.4,
                scalar2=None,
                op0=ALU.mult,
                op1=ALU.min,
                accum_out=shift[:, t : t + 1],
            )
            nc.scalar.activation(out=ha_pairs[:, t // 2, :, t % 2], in_=za[t][:], func=ACT.Relu, bias=shift[:, t : t + 1])

        hb = [sb.tile([P, P, PACK], BF16, name=f"hb{g}", tag=f"hb{g}", align_bytes=64) for g in range(2)]
        hb_codes = [sb.tile([P, P], U32, name=f"hb_codes{g}", align_bytes=64) for g in range(2)]
        hb_plane = [sb.tile([P, P], U8, name=f"hb_plane{g}", align_bytes=64) for g in range(2)]
        ha_codes = shared.tile([P, 2, P], U32, name="ha_codes", align_bytes=64, offset=0)
        ha_plane = [sb.tile([P, P], U8, name=f"ha_plane{h}", align_bytes=64) for h in range(2)]
        for g in range(2):
            nc.vector.tensor_tensor(
                out=hb[g][:].rearrange("p (c i) t -> p c t i", i=4),
                in0=zb[g][:].rearrange("p t (c i) -> p c t i", i=4),
                in1=own[:, :, P * g : P * (g + 1)].rearrange("p t (c i) -> p c t i", i=4),
                op=ALU.max,
            )
        ha = [
            sb.tile([P, P * PACK], BF16, name="ha0", align_bytes=64),
            shared.tile([P, P * PACK], BF16, name="ha1", align_bytes=64, offset=2048),
        ]
        pairs = ha_pairs[:].rearrange("p u j e -> p u (j e)")
        for h, (copy, word) in enumerate(((nc.scalar.copy, U32), (nc.vector.tensor_copy, I32))):
            copy(
                out=ha[h][:].bitcast(word).rearrange("p (j u) -> p j u", u=2),
                in_=pairs.bitcast(word)[:, :, P * h : P * (h + 1)].rearrange("p u j -> p j u"),
            )
        for h in range(2):
            nc.vector.quantize_mx(
                out=hb_codes[h][:].bitcast(E4M3), scales=hb_plane[h][:], in_=hb[h][:].rearrange("p i t -> p (i t)")
            )
            nc.vector.quantize_mx(
                out=ha_codes[:, h, :].bitcast(E5M2), scales=ha_plane[h][:], in_=ha[h][:]
            )

        factor = [
            sb.tile([P, I], F32, name=f"factor{h}", tag=tag, align_bytes=64)
            for h, tag in enumerate(("hb1", "factor1"))
        ]
        nc.vector.tensor_copy(factor[0][:], table[0][:].indirect(list_v[:]))
        nc.scalar.activation(out=factor[1][:], in_=table[1][:].indirect(list_v[:]), func=ACT.Copy)

        squashed = sb.tile([P, 2, I], F32, name="squashed", tag="table1", align_bytes=64)
        result = sb.tile([P, 2, I], F32, name="result", tag="table0", align_bytes=64)
        for h in range(2):
            for g in range(2):
                cols = slice(P * g, P * (g + 1))
                score = ps.tile([P, P], F32, name=f"za{2 * h + g}")
                nc.tensor.matmul_mx(
                    out=score[:],
                    lhsT=ha_codes[:, h, :].bitcast(E5M2),
                    lhsT_scale=ha_plane[h][:],
                    rhs=hb_codes[g][:].bitcast(E4M3),
                    rhs_scale=hb_plane[g][:],
                    start=True,
                    stop=True,
                )
                nc.scalar.activation(out=squashed[:, h, cols], in_=score[:], func=ACT.Tanh, scale=0.04)
                nc.vector.tensor_tensor(
                    out=result[:, h, cols], in0=squashed[:, h, cols], in1=factor[h][:, cols], op=ALU.mult
                )
            nc.sync.dma_start(out=out[P * h : P * (h + 1), :], in_=result[:, h, :])
